import numpy as np
import ml_dtypes


def mxq(x, axis, fmt="e4m3"):
    dtype, down = {"e4m3": (ml_dtypes.float8_e4m3fn, 7), "e5m2": (ml_dtypes.float8_e5m2, 14)}[fmt]
    v = np.moveaxis(np.asarray(x, np.float32).astype(ml_dtypes.bfloat16).astype(np.float64), axis, -1)
    blocks = v.reshape(v.shape[:-1] + (-1, 32))
    amax = np.abs(blocks).max(-1, keepdims=True)
    byte = np.maximum(np.where(amax > 0, np.frexp(amax)[1] - 1 + 127, 0) - down, 1)
    scale = np.exp2(byte - 127.0)
    codes = (blocks / scale).astype(np.float32).astype(dtype).astype(np.float64)
    return np.moveaxis((codes * scale).reshape(v.shape), -1, axis)


WIDE = False


def mx_kscale(k):
    if not WIDE:
        return np.ones(k)
    levels = np.array([30, -30])
    if k % 512:
        return np.exp2(np.random.permutation(np.resize(levels, k // 32))).repeat(32)
    a = np.empty((k // 512, 16))
    for p in range(k // 512):
        a[p, :8] = np.random.permutation(np.resize(levels, 8))
        for g in range(8):
            far = levels[np.abs(levels - a[p, g]) >= 10]
            a[p, g + 8] = far[np.random.randint(len(far))]
    return np.exp2(a.ravel()).repeat(32)


BF16 = ml_dtypes.bfloat16


def bf(x):
    return np.asarray(x, np.float32).astype(BF16)


def f64(x):
    return np.asarray(x).astype(np.float64)


M, K, R, N = 1024, 1024, 512, 2048


def setup_inputs():
    s = mx_kscale(K)
    r = mx_kscale(R)
    coef = np.random.standard_normal((M, K))
    basis = 0.5 * np.random.standard_normal((K, N)) / np.sqrt(K)
    spec = np.random.standard_t(5, (M, R))
    spec_basis = 0.4 * np.random.standard_normal((R, N)) / np.sqrt(R)
    return {"coef": bf(coef * s),
            "basis": bf(basis / s[:, None]),
            "spec": bf(spec * r),
            "spec_basis": bf(spec_basis / r[:, None]),
            "mean_log": bf(0.3 * np.random.standard_normal(N)),
            "cosine": bf(np.random.uniform(0.2, 1.0, N)),
            "light": bf(np.exp(0.4 * np.random.standard_normal((M, N))))}


def reference(coef, basis, spec, spec_basis, mean_log, cosine, light):
    principal = mxq(f64(coef), 1, "e4m3") @ mxq(f64(basis), 0, "e4m3")
    highlight = mxq(f64(spec), 1, "e5m2") @ mxq(f64(spec_basis), 0, "e4m3")
    log_rho = principal + highlight + f64(mean_log)
    return np.exp(log_rho) * f64(cosine) * f64(light)

@@ -1,0 +1,344 @@
+from contextlib import ExitStack
+
+import concourse.mybir as mybir
+from concourse.masks import make_identity
+
+M, K, R, N = 1024, 1024, 512, 2048
+FLOPS = 2 * M * (K + R) * N
+
+F32 = mybir.dt.float32
+BF16 = mybir.dt.bfloat16
+U32 = mybir.dt.uint32
+U8 = mybir.dt.uint8
+E4M3 = mybir.dt.float8_e4m3fn_x4
+E5M2 = mybir.dt.float8_e5m2_x4
+EXP = mybir.ActivationFunctionType.Exp
+MULT = mybir.AluOpType.mult
+
+P = 128
+PTS = 512
+DIRS = 512
+HEAD = 336
+SIDE = {
+    (1, 0): [("v", 1, 0, 0, 256), ("s", 1, 0, 256, 512)],
+    (1, 1): [("q", 1, 0), ("v", 1, 1, 0, 256), ("s", 1, 1, 256, 512)],
+    (1, 2): [("q", 1, 1)],
+    (1, 3): [("v", 1, 2, 0, 256), ("s", 1, 2, 256, 512)],
+    (1, 4): [("q", 1, 2)],
+    (3, 0): [("v", 2, 0, 0, 128)],
+    (3, 1): [("v", 2, 1, 0, 128)],
+    (3, 2): [("v", 2, 2, 0, 128)],
+    (3, 3): [("s", 2, 0, 128, 512), ("q", 2, 0), ("s", 2, 1, 128, 512), ("q", 2, 1), ("s", 2, 2, 128, 512), ("q", 2, 2)],
+    (4, 2): [("v", 3, 0, 0, 128)],
+    (4, 3): [("s", 3, 0, 128, 512)],
+    (5, 0): [("q", 3, 0)],
+    (5, 1): [("v", 3, 1, 0, 128)],
+    (5, 2): [("v", 3, 2, 0, 128)],
+    (5, 3): [("s", 3, 1, 128, 512), ("s", 3, 2, 128, 512)],
+    (5, 4): [("q", 3, 1), ("q", 3, 2)],
+}
+
+
+def tile_log_brdf_light_s2_kernel(tc, coef, basis, spec, spec_basis, mean_log, cosine, light, out):
+    nc = tc.nc
+    with ExitStack() as ctx:
+        keep = ctx.enter_context(tc.tile_pool(name="keep", bufs=1))
+        grp = ctx.enter_context(tc.tile_pool(name="grp", bufs=4))
+        work = ctx.enter_context(tc.tile_pool(name="work", bufs=8))
+        outs = ctx.enter_context(tc.tile_pool(name="outs", bufs=4))
+        psum = ctx.enter_context(tc.psum_pool(name="psum", bufs=4))
+        ctx.enter_context(tc.manual_schedule(engines={mybir.EngineType.PE, mybir.EngineType.SP}))
+
+        def fixed(shape, dtype, name):
+            return keep.tile(shape, dtype, name=name, align_bytes=64)
+
+        ident = fixed([P, P], F32, "ident")
+        mc_rows = fixed([P, P], BF16, "mc_rows")
+        mc_f32 = fixed([P, P], F32, "mc_f32")
+        mc = fixed([P, 32], F32, "mc")
+        warm = fixed([P, 8], F32, "warm")
+        nc.vector.memset(warm[:], 0.0)
+        nc.vector.memset(mc_rows[:], 0.0)
+        nc.scalar.activation(out=warm[:], in_=warm[:], func=EXP)
+        make_identity(nc, ident[:])
+
+        coef_raw, spec_raw, dir_raw, light_raw = {}, {}, {}, {}
+
+        def load_coef(h, g):
+            t = fixed([P, 4, 512], BF16, "coef_%d_%d" % (h, g))
+            src = coef[h * PTS : (h + 1) * PTS, 512 * g : 512 * (g + 1)]
+            nc.sync.dma_start(out=t[:], in_=src.rearrange("(p j) k -> p j k", j=4))
+            coef_raw[h, g] = t
+
+        def load_spec(h):
+            t = fixed([P, 4, R], BF16, "spec_%d" % h)
+            nc.sync.dma_start(out=t[:], in_=spec[h * PTS : (h + 1) * PTS, :].rearrange("(p j) k -> p j k", j=4))
+            spec_raw[h] = t
+
+        def load_dirs(g, c0, c1):
+            t = fixed([P, 4, c1 - c0], BF16, "dirs_%d_%d" % (g, c0))
+            src = basis[g * 512 : (g + 1) * 512, c0:c1] if g < 2 else spec_basis[:, c0:c1]
+            nc.sync.dma_start(out=t[:], in_=src.rearrange("(p j) n -> p j n", j=4))
+            for b in range(c0 // DIRS, c1 // DIRS):
+                dir_raw[b, g] = t[:, :, b * DIRS - c0 : (b + 1) * DIRS - c0]
+
+        def load_light(h, c0, c1):
+            t = fixed([P, 4, c1 - c0], BF16, "light_%d_%d" % (h, c0))
+            src = light[h * PTS : (h + 1) * PTS, c0:c1]
+            nc.sync.dma_start(out=t[:], in_=src.rearrange("(p j) n -> p j n", j=4))
+            for q in range(c0 // P, c1 // P):
+                light_raw[h, q] = t[:, :, q * P - c0 : (q + 1) * P - c0]
+
+        load_coef(0, 0)
+        load_dirs(0, 0, 512)
+        nc.sync.dma_start(out=mc_rows[0:16, :], in_=mean_log.rearrange("(t p) -> t p", p=P))
+        nc.sync.dma_start(out=mc_rows[16:32, :], in_=cosine.rearrange("(t p) -> t p", p=P))
+        load_coef(0, 1)
+        load_dirs(1, 0, 512)
+        load_spec(0)
+        load_dirs(2, 0, 512)
+        load_coef(1, 0)
+        load_coef(1, 1)
+        load_spec(1)
+        load_light(0, 0, 1024)
+        load_dirs(0, 512, 1024)
+        load_dirs(1, 512, 1024)
+        load_dirs(2, 512, 1024)
+        load_light(1, 0, 1024)
+        load_dirs(0, 1024, 2048)
+        load_dirs(1, 1024, 2048)
+        load_dirs(2, 1024, 2048)
+        load_light(0, 1024, 2048)
+        load_light(1, 1024, 2048)
+
+        codes, scales, grouped = {}, {}, {}
+
+        def group(key):
+            if key not in grouped:
+                grouped[key] = grp.tile([P, 512, 4], BF16, name="grouped", align_bytes=64)
+            return grouped[key]
+
+        def quantize(key, fmt=E4M3):
+            tag = "_".join(str(x) for x in key)
+            codes[key] = fixed([P, 512], U32, "codes_" + tag)
+            scales[key] = fixed([P, 512], U8, "scales_" + tag)
+            nc.vector.quantize_mx(
+                out=codes[key][:].bitcast(fmt),
+                scales=scales[key][:],
+                in_=grouped[key][:].rearrange("p n t -> p (n t)"),
+            )
+
+        def interleave(engine_copy, b, g, c0, c1):
+            engine_copy(
+                out=group(("d", b, g))[:, c0:c1, :].rearrange("p (c i) t -> p c t i", i=4),
+                in_=dir_raw[b, g][:, :, c0:c1].rearrange("p t (c i) -> p c t i", i=4),
+            )
+
+        banks = {}
+
+        def sort_words(engine_copy, key, raw):
+            t = fixed([P, 4, 2, P], F32, "sorted_" + "_".join(str(x) for x in key))
+            engine_copy(
+                out=t[:],
+                in_=raw.rearrange("p j k -> p (j k)").bitcast(F32).rearrange("p (j q u) -> p j u q", j=4, u=2),
+            )
+            sorted_words[key] = t
+
+        sorted_words = {}
+
+        def turn_sorted(key, src_key, jp):
+            bank = psum.tile([P, 512], F32, name="turned")
+            for j in range(2):
+                for u in range(2):
+                    nc.tensor.transpose(
+                        bank[:, (2 * j + u) * P : (2 * j + u + 1) * P],
+                        sorted_words[src_key][:, 2 * jp + j, u, :],
+                        ident[:],
+                    )
+            banks[key] = bank
+
+        def turn(key, tile, k_words, j0, word0):
+            bank = psum.tile([P, 512], F32, name="turned")
+            words = tile.rearrange("p j k -> p (j k)").bitcast(F32)
+            for j in range(2):
+                for u in range(2):
+                    base = (j0 + j) * k_words + word0 + u
+                    nc.tensor.transpose(
+                        bank[:, (2 * j + u) * P : (2 * j + u + 1) * P],
+                        words[:, base : base + 255 : 2],
+                        ident[:],
+                    )
+            banks[key] = bank
+
+        def collect(engine_copy, key, bank_key, jp):
+            engine_copy(
+                out=group(key)[:]
+                .rearrange("p n t -> p (n t)")
+                .bitcast(F32)[:, jp * 512 : (jp + 1) * 512]
+                .rearrange("p (j r u) -> p j r u", j=2, u=2),
+                in_=banks[bank_key][:].rearrange("p (j u r) -> p j r u", j=2, u=2),
+            )
+
+        vcopy, scopy = nc.vector.tensor_copy, nc.scalar.copy
+
+        acc, e = {}, {}
+
+        def matmul(h, q, g):
+            if g == 0:
+                acc[h, q] = psum.tile([P, PTS], F32, name="acc")
+            b, c = q // 4, (q % 4) * P
+            pts = ("s", h) if g == 2 else ("c", h, g)
+            nc.tensor.matmul_mx(
+                out=acc[h, q][:],
+                lhsT=codes["d", b, g][:, c : c + P].bitcast(E4M3),
+                lhsT_scale=scales["d", b, g][:, c : c + P],
+                rhs=codes[pts][:].bitcast(E5M2 if g == 2 else E4M3),
+                rhs_scale=scales[pts][:],
+                start=(g == 0),
+                stop=(g == 2),
+            )
+
+        def expo(h, q):
+            e[h, q] = work.tile([P, PTS], F32, name="e")
+            nc.scalar.activation(out=e[h, q][:], in_=acc[h, q][:], func=EXP, bias=mc[:, q : q + 1])
+
+        def cosi(h, q):
+            nc.vector.tensor_scalar(
+                out=e[h, q][:], in0=e[h, q][:], scalar1=mc[:, 16 + q : 17 + q], scalar2=None, op0=MULT
+            )
+
+        def back(h, q):
+            bank = psum.tile([P, 512], F32, name="turned")
+            for j in range(4):
+                nc.tensor.transpose(bank[:, j * P : (j + 1) * P], e[h, q][:, j * P : (j + 1) * P], ident[:])
+            banks["out", h, q] = bank
+
+        out_tiles = {}
+
+        def finish(h, q):
+            b = q // 4
+            if q % 4 == 0:
+                out_tiles[h, b] = outs.tile([P, 4, DIRS], F32, name="o")
+            c = (q % 4) * P
+            nc.vector.tensor_tensor(
+                out=out_tiles[h, b][:, :, c : c + P],
+                in0=banks["out", h, q][:].rearrange("p (j d) -> p j d", j=4),
+                in1=light_raw[h, q],
+                op=MULT,
+            )
+
+        def store(h, b, c0, c1):
+            dst = out[h * PTS : (h + 1) * PTS, b * DIRS + c0 : b * DIRS + c1]
+            nc.sync.dma_start(out=dst.rearrange("(p j) n -> p j n", j=4), in_=out_tiles[h, b][:, :, c0:c1])
+
+        def turn_coef(h, g, jp):
+            turn(("c", h, g, jp), coef_raw[h, g][:], 256, 2 * jp, 0)
+
+        def turn_spec(h, jp):
+            turn(("s", h, jp), spec_raw[h][:], 256, 2 * jp, 0)
+
+        def side(i, j):
+            for kind, b, g, *cols in SIDE.get((i, j), []):
+                if kind == "q":
+                    quantize(("d", b, g))
+                else:
+                    interleave(vcopy if kind == "v" else scopy, b, g, *cols)
+
+        def dirs_head(g):
+            interleave(vcopy, 0, g, 0, HEAD)
+            interleave(scopy, 0, g, HEAD, 512)
+
+        def points_head(h, g, engines):
+            for jp in range(2):
+                turn_coef(h, g, jp)
+            for jp in range(2):
+                collect(engines[jp], ("c", h, g), ("c", h, g, jp), jp)
+
+        points_head(0, 0, (scopy, vcopy))
+        quantize(("c", 0, 0))
+        dirs_head(0)
+        nc.vector.tensor_copy(out=mc_f32[:], in_=mc_rows[:])
+        quantize(("d", 0, 0))
+        points_head(0, 1, (scopy, vcopy))
+        mc_bank = psum.tile([P, 512], F32, name="turned")
+        nc.tensor.transpose(mc_bank[:, 0:P], mc_f32[:], ident[:])
+        nc.vector.tensor_copy(out=mc[:], in_=mc_bank[:, 0:32])
+        for q in range(4):
+            matmul(0, q, 0)
+        quantize(("c", 0, 1))
+        dirs_head(1)
+        quantize(("d", 0, 1))
+        turn_spec(0, 0)
+        turn_spec(0, 1)
+        collect(scopy, ("s", 0), ("s", 0, 0), 0)
+        collect(vcopy, ("s", 0), ("s", 0, 1), 1)
+        for q in range(4):
+            matmul(0, q, 1)
+        quantize(("s", 0), E5M2)
+        dirs_head(2)
+        quantize(("d", 0, 2))
+        for q in range(4):
+            matmul(0, q, 2)
+
+        sort_words(scopy, ("c", 1, 0), coef_raw[1, 0][:])
+        sort_words(vcopy, ("c", 1, 1), coef_raw[1, 1][:])
+        sort_words(vcopy, ("s", 1), spec_raw[1][:])
+        for q in range(4):
+            expo(0, q)
+        for key in (("c", 1, 0), ("c", 1, 1), ("s", 1)):
+            for jp in range(2):
+                turn_sorted(key + (jp,), key, jp)
+            for jp in range(2):
+                collect(scopy if jp else vcopy, key, key + (jp,), jp)
+            quantize(key, E5M2 if key[0] == "s" else E4M3)
+        for q in range(4):
+            cosi(0, q)
+
+        def units(i):
+            return [(i % 2, 4 * (i // 2) + j) for j in range(4)]
+
+        def unit(i, j):
+            h, q = units(i)[j]
+            for g in range(3):
+                matmul(h, q, g)
+            expo(h, q)
+            cosi(h, q)
+            side(i, j)
+
+        def give_back(i):
+            for u in units(i):
+                back(*u)
+            for u in units(i):
+                finish(*u)
+
+        for q in range(4):
+            matmul(1, q, 0)
+        give_back(0)
+        store(0, 0, 0, 512)
+        for g in (1, 2):
+            for q in range(4):
+                matmul(1, q, g)
+        for q in range(4):
+            expo(1, q)
+            cosi(1, q)
+            side(1, q)
+        side(1, 4)
+        for i in range(2, 7):
+            for j in range(4):
+                unit(i, j)
+            give_back(i - 1)
+            store((i - 1) % 2, (i - 1) // 2, 0, 512)
+            side(i, 4)
+        unit(7, 0)
+        unit(7, 1)
+        give_back(6)
+        store(0, 3, 0, 512)
+        unit(7, 2)
+        unit(7, 3)
+        for j in range(4):
+            back(*units(7)[j])
+            finish(*units(7)[j])
+            if j == 1:
+                store(1, 3, 0, 256)
+            elif j > 1:
+                store(1, 3, 128 * j, 128 * j + 128)

@@ -14,331 +14,357 @@ E4M3 = mybir.dt.float8_e4m3fn_x4
 E5M2 = mybir.dt.float8_e5m2_x4
 EXP = mybir.ActivationFunctionType.Exp
 MULT = mybir.AluOpType.mult
+ADD = mybir.AluOpType.add
 
 P = 128
-PTS = 512
-DIRS = 512
-HEAD = 336
-SIDE = {
-    (1, 0): [("v", 1, 0, 0, 256), ("s", 1, 0, 256, 512)],
-    (1, 1): [("q", 1, 0), ("v", 1, 1, 0, 256), ("s", 1, 1, 256, 512)],
-    (1, 2): [("q", 1, 1)],
-    (1, 3): [("v", 1, 2, 0, 256), ("s", 1, 2, 256, 512)],
-    (1, 4): [("q", 1, 2)],
-    (3, 0): [("v", 2, 0, 0, 128)],
-    (3, 1): [("v", 2, 1, 0, 128)],
-    (3, 2): [("v", 2, 2, 0, 128)],
-    (3, 3): [("s", 2, 0, 128, 512), ("q", 2, 0), ("s", 2, 1, 128, 512), ("q", 2, 1), ("s", 2, 2, 128, 512), ("q", 2, 2)],
-    (4, 2): [("v", 3, 0, 0, 128)],
-    (4, 3): [("s", 3, 0, 128, 512)],
-    (5, 0): [("q", 3, 0)],
-    (5, 1): [("v", 3, 1, 0, 128)],
-    (5, 2): [("v", 3, 2, 0, 128)],
-    (5, 3): [("s", 3, 1, 128, 512), ("s", 3, 2, 128, 512)],
-    (5, 4): [("q", 3, 1), ("q", 3, 2)],
-}
+J = 4
+W = 512
+
+SPECULAR = 2
+PASSES = 3
+
+RUNS = [(0, 0), (1, 0), (0, 1), (1, 1), (0, 2), (1, 2), (0, 3), (1, 3)]
+
+VECTOR_COLUMNS = [(336, 336, 336), (192, 320, 320), (192, 320, 192), (96, 256, 192)]
 
 
 def tile_log_brdf_light_s2_kernel(tc, coef, basis, spec, spec_basis, mean_log, cosine, light, out):
     nc = tc.nc
+    vector_copy, scalar_copy = nc.vector.tensor_copy, nc.scalar.copy
+
     with ExitStack() as ctx:
         keep = ctx.enter_context(tc.tile_pool(name="keep", bufs=1))
-        grp = ctx.enter_context(tc.tile_pool(name="grp", bufs=4))
-        work = ctx.enter_context(tc.tile_pool(name="work", bufs=8))
-        outs = ctx.enter_context(tc.tile_pool(name="outs", bufs=4))
+        grouped_pool = ctx.enter_context(tc.tile_pool(name="grouped", bufs=4))
+        exp_pool = ctx.enter_context(tc.tile_pool(name="exp", bufs=8))
+        out_pool = ctx.enter_context(tc.tile_pool(name="out", bufs=4))
         psum = ctx.enter_context(tc.psum_pool(name="psum", bufs=4))
-        ctx.enter_context(tc.manual_schedule(engines={mybir.EngineType.PE, mybir.EngineType.SP}))
+        ctx.enter_context(tc.manual_schedule())
 
         def fixed(shape, dtype, name):
             return keep.tile(shape, dtype, name=name, align_bytes=64)
 
-        ident = fixed([P, P], F32, "ident")
-        mc_rows = fixed([P, P], BF16, "mc_rows")
-        mc_f32 = fixed([P, P], F32, "mc_f32")
-        mc = fixed([P, 32], F32, "mc")
-        warm = fixed([P, 8], F32, "warm")
-        nc.vector.memset(warm[:], 0.0)
-        nc.vector.memset(mc_rows[:], 0.0)
-        nc.scalar.activation(out=warm[:], in_=warm[:], func=EXP)
-        make_identity(nc, ident[:])
+        def by_four(rows):
+            return rows.rearrange("(p j) w -> p j w", j=J)
 
-        coef_raw, spec_raw, dir_raw, light_raw = {}, {}, {}, {}
+        points, dirs, light_in = {}, {}, {}
 
-        def load_coef(h, g):
-            t = fixed([P, 4, 512], BF16, "coef_%d_%d" % (h, g))
-            src = coef[h * PTS : (h + 1) * PTS, 512 * g : 512 * (g + 1)]
-            nc.sync.dma_start(out=t[:], in_=src.rearrange("(p j) k -> p j k", j=4))
-            coef_raw[h, g] = t
+        def load_coef(h, k0, k1):
+            t = fixed([P, J, k1 - k0], BF16, "coef_%d_%d" % (h, k0))
+            nc.sync.dma_start(out=t[:], in_=by_four(coef[h * W : (h + 1) * W, k0:k1]))
+            for g in range(k0 // W, k1 // W):
+                points[h, g] = t[:, :, g * W - k0 : (g + 1) * W - k0]
 
         def load_spec(h):
-            t = fixed([P, 4, R], BF16, "spec_%d" % h)
-            nc.sync.dma_start(out=t[:], in_=spec[h * PTS : (h + 1) * PTS, :].rearrange("(p j) k -> p j k", j=4))
-            spec_raw[h] = t
+            t = fixed([P, J, R], BF16, "spec_%d" % h)
+            nc.sync.dma_start(out=t[:], in_=by_four(spec[h * W : (h + 1) * W, :]))
+            points[h, SPECULAR] = t[:]
 
-        def load_dirs(g, c0, c1):
-            t = fixed([P, 4, c1 - c0], BF16, "dirs_%d_%d" % (g, c0))
-            src = basis[g * 512 : (g + 1) * 512, c0:c1] if g < 2 else spec_basis[:, c0:c1]
-            nc.sync.dma_start(out=t[:], in_=src.rearrange("(p j) n -> p j n", j=4))
-            for b in range(c0 // DIRS, c1 // DIRS):
-                dir_raw[b, g] = t[:, :, b * DIRS - c0 : (b + 1) * DIRS - c0]
+        def load_dirs(g, n0, n1):
+            t = fixed([P, J, n1 - n0], BF16, "dirs_%d_%d" % (g, n0))
+            rows = spec_basis if g == SPECULAR else basis[g * W : (g + 1) * W, :]
+            nc.sync.dma_start(out=t[:], in_=by_four(rows[:, n0:n1]))
+            for b in range(n0 // W, n1 // W):
+                dirs[b, g] = t[:, :, b * W - n0 : (b + 1) * W - n0]
 
-        def load_light(h, c0, c1):
-            t = fixed([P, 4, c1 - c0], BF16, "light_%d_%d" % (h, c0))
-            src = light[h * PTS : (h + 1) * PTS, c0:c1]
-            nc.sync.dma_start(out=t[:], in_=src.rearrange("(p j) n -> p j n", j=4))
-            for q in range(c0 // P, c1 // P):
-                light_raw[h, q] = t[:, :, q * P - c0 : (q + 1) * P - c0]
+        def load_light(h, n0, n1):
+            t = fixed([P, J, n1 - n0], BF16, "light_%d_%d" % (h, n0))
+            nc.sync.dma_start(out=t[:], in_=by_four(light[h * W : (h + 1) * W, n0:n1]))
+            for q in range(n0 // P, n1 // P):
+                light_in[h, q] = t[:, :, q * P - n0 : (q + 1) * P - n0]
 
-        load_coef(0, 0)
-        load_dirs(0, 0, 512)
-        nc.sync.dma_start(out=mc_rows[0:16, :], in_=mean_log.rearrange("(t p) -> t p", p=P))
-        nc.sync.dma_start(out=mc_rows[16:32, :], in_=cosine.rearrange("(t p) -> t p", p=P))
-        load_coef(0, 1)
-        load_dirs(1, 0, 512)
+        vectors = fixed([P, P], BF16, "vectors")
+        nc.vector.memset(vectors[:], 0.0)
+
+        load_coef(0, 0, W)
+        load_dirs(0, 0, W)
+        nc.sync.dma_start(out=vectors[0:16, :], in_=mean_log.rearrange("(t p) -> t p", p=P))
+        nc.sync.dma_start(out=vectors[16:32, :], in_=cosine.rearrange("(t p) -> t p", p=P))
+        load_coef(0, W, K)
+        load_dirs(1, 0, W)
         load_spec(0)
-        load_dirs(2, 0, 512)
-        load_coef(1, 0)
-        load_coef(1, 1)
+        load_dirs(SPECULAR, 0, W)
+        load_coef(1, 0, K)
         load_spec(1)
-        load_light(0, 0, 1024)
-        load_dirs(0, 512, 1024)
-        load_dirs(1, 512, 1024)
-        load_dirs(2, 512, 1024)
-        load_light(1, 0, 1024)
-        load_dirs(0, 1024, 2048)
-        load_dirs(1, 1024, 2048)
-        load_dirs(2, 1024, 2048)
-        load_light(0, 1024, 2048)
-        load_light(1, 1024, 2048)
+        load_light(0, 0, W)
+        for g in range(PASSES):
+            load_dirs(g, W, 2 * W)
+        load_light(1, 0, W)
+        for g in range(PASSES):
+            load_dirs(g, 2 * W, N)
+        load_light(0, W, N)
+        load_light(1, W, N)
 
-        codes, scales, grouped = {}, {}, {}
+        grouped, codes, scales, banks, split = {}, {}, {}, {}, {}
 
         def group(key):
             if key not in grouped:
-                grouped[key] = grp.tile([P, 512, 4], BF16, name="grouped", align_bytes=64)
+                grouped[key] = grouped_pool.tile([P, W, J], BF16, name="grouped", align_bytes=64)
             return grouped[key]
 
-        def quantize(key, fmt=E4M3):
-            tag = "_".join(str(x) for x in key)
-            codes[key] = fixed([P, 512], U32, "codes_" + tag)
-            scales[key] = fixed([P, 512], U8, "scales_" + tag)
+        def quantize(key):
+            name = "%s_%d_%d" % key
+            codes[key] = fixed([P, W], U32, "codes_" + name)
+            scales[key] = fixed([P, W], U8, "scales_" + name)
             nc.vector.quantize_mx(
-                out=codes[key][:].bitcast(fmt),
+                out=codes[key][:].bitcast(code_type(key)),
                 scales=scales[key][:],
-                in_=grouped[key][:].rearrange("p n t -> p (n t)"),
+                in_=group(key)[:].rearrange("p n t -> p (n t)"),
             )
 
-        def interleave(engine_copy, b, g, c0, c1):
+        def code_type(key):
+            return E5M2 if key[0] == "points" and key[2] == SPECULAR else E4M3
+
+        def interleave(engine_copy, b, g, n0, n1):
             engine_copy(
-                out=group(("d", b, g))[:, c0:c1, :].rearrange("p (c i) t -> p c t i", i=4),
-                in_=dir_raw[b, g][:, :, c0:c1].rearrange("p t (c i) -> p c t i", i=4),
+                out=group(("dirs", b, g))[:, n0:n1, :].rearrange("p (c i) t -> p c t i", i=4),
+                in_=dirs[b, g][:, :, n0:n1].rearrange("p t (c i) -> p c t i", i=4),
             )
 
-        banks = {}
+        def interleave_vector(b, g):
+            interleave(vector_copy, b, g, 0, VECTOR_COLUMNS[b][g])
 
-        def sort_words(engine_copy, key, raw):
-            t = fixed([P, 4, 2, P], F32, "sorted_" + "_".join(str(x) for x in key))
+        def interleave_scalar(b, g):
+            interleave(scalar_copy, b, g, VECTOR_COLUMNS[b][g], W)
+
+        def words(h, g):
+            return points[h, g].bitcast(F32)
+
+        def split_words(engine_copy, h, g):
+            split[h, g] = fixed([P, J, 2, P], F32, "split_%d_%d" % (h, g))
+            engine_copy(out=split[h, g][:], in_=words(h, g).rearrange("p j (q u) -> p j u q", u=2))
+
+        def turn(h, g):
+            for half in range(2):
+                bank = psum.tile([P, W], F32, name="turned")
+                for j in range(2):
+                    for u in range(2):
+                        row = 2 * half + j
+                        if (h, g) in split:
+                            source = split[h, g][:, row, u, :]
+                        else:
+                            source = words(h, g)[:, row, u::2]
+                        spot = (2 * j + u) * P
+                        nc.tensor.transpose(bank[:, spot : spot + P], source, ident[:])
+                banks["points", h, g, half] = bank
+
+        def gather(engine_copy, h, g, half):
             engine_copy(
-                out=t[:],
-                in_=raw.rearrange("p j k -> p (j k)").bitcast(F32).rearrange("p (j q u) -> p j u q", j=4, u=2),
-            )
-            sorted_words[key] = t
-
-        sorted_words = {}
-
-        def turn_sorted(key, src_key, jp):
-            bank = psum.tile([P, 512], F32, name="turned")
-            for j in range(2):
-                for u in range(2):
-                    nc.tensor.transpose(
-                        bank[:, (2 * j + u) * P : (2 * j + u + 1) * P],
-                        sorted_words[src_key][:, 2 * jp + j, u, :],
-                        ident[:],
-                    )
-            banks[key] = bank
-
-        def turn(key, tile, k_words, j0, word0):
-            bank = psum.tile([P, 512], F32, name="turned")
-            words = tile.rearrange("p j k -> p (j k)").bitcast(F32)
-            for j in range(2):
-                for u in range(2):
-                    base = (j0 + j) * k_words + word0 + u
-                    nc.tensor.transpose(
-                        bank[:, (2 * j + u) * P : (2 * j + u + 1) * P],
-                        words[:, base : base + 255 : 2],
-                        ident[:],
-                    )
-            banks[key] = bank
-
-        def collect(engine_copy, key, bank_key, jp):
-            engine_copy(
-                out=group(key)[:]
+                out=group(("points", h, g))[:]
                 .rearrange("p n t -> p (n t)")
-                .bitcast(F32)[:, jp * 512 : (jp + 1) * 512]
+                .bitcast(F32)[:, half * W : (half + 1) * W]
                 .rearrange("p (j r u) -> p j r u", j=2, u=2),
-                in_=banks[bank_key][:].rearrange("p (j u r) -> p j r u", j=2, u=2),
+                in_=banks["points", h, g, half][:].rearrange("p (j u r) -> p j r u", j=2, u=2),
             )
 
-        vcopy, scopy = nc.vector.tensor_copy, nc.scalar.copy
+        acc, e, outs = {}, {}, {}
 
-        acc, e = {}, {}
-
-        def matmul(h, q, g):
+        def multiply(h, q, g):
             if g == 0:
-                acc[h, q] = psum.tile([P, PTS], F32, name="acc")
-            b, c = q // 4, (q % 4) * P
-            pts = ("s", h) if g == 2 else ("c", h, g)
+                acc[h, q] = psum.tile([P, W], F32, name="acc")
+            d, p = ("dirs", q // 4, g), ("points", h, g)
+            c = (q % 4) * P
             nc.tensor.matmul_mx(
                 out=acc[h, q][:],
-                lhsT=codes["d", b, g][:, c : c + P].bitcast(E4M3),
-                lhsT_scale=scales["d", b, g][:, c : c + P],
-                rhs=codes[pts][:].bitcast(E5M2 if g == 2 else E4M3),
-                rhs_scale=scales[pts][:],
+                lhsT=codes[d][:, c : c + P].bitcast(code_type(d)),
+                lhsT_scale=scales[d][:, c : c + P],
+                rhs=codes[p][:].bitcast(code_type(p)),
+                rhs_scale=scales[p][:],
                 start=(g == 0),
-                stop=(g == 2),
+                stop=(g == PASSES - 1),
             )
 
-        def expo(h, q):
-            e[h, q] = work.tile([P, PTS], F32, name="e")
-            nc.scalar.activation(out=e[h, q][:], in_=acc[h, q][:], func=EXP, bias=mc[:, q : q + 1])
+        def exponential(h, q):
+            e[h, q] = exp_pool.tile([P, W], F32, name="e")
+            nc.scalar.activation(out=e[h, q][:], in_=acc[h, q][:], func=EXP, bias=columns[:, q : q + 1])
 
-        def cosi(h, q):
+        def times_cosine_gpsimd(h, q):
+            nc.gpsimd.tensor_scalar(
+                out=e[h, q][:], in0=e[h, q][:], scalar1=columns[:, 16 + q : 17 + q], scalar2=0.0, op0=MULT, op1=ADD
+            )
+
+        def times_cosine_vector(h, q):
             nc.vector.tensor_scalar(
-                out=e[h, q][:], in0=e[h, q][:], scalar1=mc[:, 16 + q : 17 + q], scalar2=None, op0=MULT
+                out=e[h, q][:], in0=e[h, q][:], scalar1=columns[:, 16 + q : 17 + q], scalar2=None, op0=MULT
             )
 
-        def back(h, q):
-            bank = psum.tile([P, 512], F32, name="turned")
-            for j in range(4):
+        def turn_back(h, q):
+            bank = psum.tile([P, W], F32, name="turned")
+            for j in range(J):
                 nc.tensor.transpose(bank[:, j * P : (j + 1) * P], e[h, q][:, j * P : (j + 1) * P], ident[:])
             banks["out", h, q] = bank
 
-        out_tiles = {}
-
-        def finish(h, q):
-            b = q // 4
-            if q % 4 == 0:
-                out_tiles[h, b] = outs.tile([P, 4, DIRS], F32, name="o")
-            c = (q % 4) * P
+        def times_light(h, q):
+            b, c = q // 4, (q % 4) * P
+            if (h, b) not in outs:
+                outs[h, b] = out_pool.tile([P, J, W], F32, name="o")
             nc.vector.tensor_tensor(
-                out=out_tiles[h, b][:, :, c : c + P],
-                in0=banks["out", h, q][:].rearrange("p (j d) -> p j d", j=4),
-                in1=light_raw[h, q],
+                out=outs[h, b][:, :, c : c + P],
+                in0=banks["out", h, q][:].rearrange("p (j n) -> p j n", j=J),
+                in1=light_in[h, q],
                 op=MULT,
             )
 
         def store(h, b, c0, c1):
-            dst = out[h * PTS : (h + 1) * PTS, b * DIRS + c0 : b * DIRS + c1]
-            nc.sync.dma_start(out=dst.rearrange("(p j) n -> p j n", j=4), in_=out_tiles[h, b][:, :, c0:c1])
+            rows = out[h * W : (h + 1) * W, b * W + c0 : b * W + c1]
+            nc.sync.dma_start(out=by_four(rows), in_=outs[h, b][:, :, c0:c1])
 
-        def turn_coef(h, g, jp):
-            turn(("c", h, g, jp), coef_raw[h, g][:], 256, 2 * jp, 0)
+        ident = fixed([P, P], F32, "ident")
+        make_identity(nc, ident[:])
+        columns = fixed([P, 32], F32, "columns")
+        first = fixed([P, 8], F32, "first")
+        nc.vector.memset(first[:], 0.0)
+        nc.scalar.activation(out=first[:], in_=first[:], func=EXP)
+        idle = ("idle", 0, 0)
+        nc.vector.memset(group(idle)[:], 0.0)
+        quantize(idle)
 
-        def turn_spec(h, jp):
-            turn(("s", h, jp), spec_raw[h][:], 256, 2 * jp, 0)
+        def keep_clock(n):
+            bank = psum.tile([P, W], F32, name="turned")
+            for i in range(n):
+                nc.tensor.matmul_mx(
+                    out=bank[:],
+                    lhsT=codes[idle][:, 0:P].bitcast(E4M3),
+                    lhsT_scale=scales[idle][:, 0:P],
+                    rhs=codes[idle][:].bitcast(E4M3),
+                    rhs_scale=scales[idle][:],
+                    start=(i == 0),
+                    stop=(i == n - 1),
+                )
 
-        def side(i, j):
-            for kind, b, g, *cols in SIDE.get((i, j), []):
-                if kind == "q":
-                    quantize(("d", b, g))
-                else:
-                    interleave(vcopy if kind == "v" else scopy, b, g, *cols)
+        def pass_of_run(h, b, g):
+            for q in range(4 * b, 4 * b + 4):
+                multiply(h, q, g)
 
-        def dirs_head(g):
-            interleave(vcopy, 0, g, 0, HEAD)
-            interleave(scopy, 0, g, HEAD, 512)
-
-        def points_head(h, g, engines):
-            for jp in range(2):
-                turn_coef(h, g, jp)
-            for jp in range(2):
-                collect(engines[jp], ("c", h, g), ("c", h, g, jp), jp)
-
-        points_head(0, 0, (scopy, vcopy))
-        quantize(("c", 0, 0))
-        dirs_head(0)
-        nc.vector.tensor_copy(out=mc_f32[:], in_=mc_rows[:])
-        quantize(("d", 0, 0))
-        points_head(0, 1, (scopy, vcopy))
-        mc_bank = psum.tile([P, 512], F32, name="turned")
-        nc.tensor.transpose(mc_bank[:, 0:P], mc_f32[:], ident[:])
-        nc.vector.tensor_copy(out=mc[:], in_=mc_bank[:, 0:32])
+        turn(0, 0)
+        gather(scalar_copy, 0, 0, 0)
+        gather(scalar_copy, 0, 0, 1)
+        interleave_vector(0, 0)
+        interleave_scalar(0, 0)
+        quantize(("points", 0, 0))
+        turn(0, 1)
+        wide = fixed([P, P], F32, "wide")
+        nc.vector.tensor_copy(out=wide[:], in_=vectors[:])
+        quantize(("dirs", 0, 0))
+        columns_bank = psum.tile([P, W], F32, name="turned")
+        nc.tensor.transpose(columns_bank[:, 0:P], wide[:], ident[:])
+        gather(scalar_copy, 0, 1, 0)
+        gather(scalar_copy, 0, 1, 1)
+        pass_of_run(0, 0, 0)
+        interleave_vector(0, 1)
+        interleave_scalar(0, 1)
+        quantize(("points", 0, 1))
+        nc.vector.tensor_copy(out=columns[:], in_=columns_bank[:, 0:32])
+        quantize(("dirs", 0, 1))
+        turn(0, SPECULAR)
+        pass_of_run(0, 0, 1)
+        interleave_vector(0, SPECULAR)
+        interleave_scalar(0, SPECULAR)
+        gather(vector_copy, 0, SPECULAR, 1)
+        gather(scalar_copy, 0, SPECULAR, 0)
+        quantize(("dirs", 0, SPECULAR))
+        quantize(("points", 0, SPECULAR))
+        split_words(scalar_copy, 1, 1)
+        turn(1, 0)
+        pass_of_run(0, 0, SPECULAR)
+        gather(vector_copy, 1, 0, 0)
+        gather(scalar_copy, 1, 0, 1)
+        split_words(vector_copy, 1, SPECULAR)
+        turn(1, 1)
         for q in range(4):
-            matmul(0, q, 0)
-        quantize(("c", 0, 1))
-        dirs_head(1)
-        quantize(("d", 0, 1))
-        turn_spec(0, 0)
-        turn_spec(0, 1)
-        collect(scopy, ("s", 0), ("s", 0, 0), 0)
-        collect(vcopy, ("s", 0), ("s", 0, 1), 1)
+            exponential(0, q)
+        quantize(("points", 1, 0))
+        pass_of_run(1, 0, 0)
+        gather(vector_copy, 1, 1, 0)
+        gather(scalar_copy, 1, 1, 1)
+        turn(1, SPECULAR)
+        times_cosine_gpsimd(0, 0)
+        times_cosine_gpsimd(0, 1)
+        times_cosine_vector(0, 2)
+        times_cosine_gpsimd(0, 3)
+        interleave_vector(1, 0)
+        interleave_scalar(1, 0)
+        quantize(("points", 1, 1))
+        gather(vector_copy, 1, SPECULAR, 0)
+        gather(scalar_copy, 1, SPECULAR, 1)
+        keep_clock(2)
         for q in range(4):
-            matmul(0, q, 1)
-        quantize(("s", 0), E5M2)
-        dirs_head(2)
-        quantize(("d", 0, 2))
+            turn_back(0, q)
+        pass_of_run(1, 0, 1)
+        interleave_vector(1, 1)
+        interleave_scalar(1, 1)
+        quantize(("points", 1, SPECULAR))
+        interleave_vector(1, SPECULAR)
+        interleave_scalar(1, SPECULAR)
+        pass_of_run(1, 0, SPECULAR)
         for q in range(4):
-            matmul(0, q, 2)
-
-        sort_words(scopy, ("c", 1, 0), coef_raw[1, 0][:])
-        sort_words(vcopy, ("c", 1, 1), coef_raw[1, 1][:])
-        sort_words(vcopy, ("s", 1), spec_raw[1][:])
-        for q in range(4):
-            expo(0, q)
-        for key in (("c", 1, 0), ("c", 1, 1), ("s", 1)):
-            for jp in range(2):
-                turn_sorted(key + (jp,), key, jp)
-            for jp in range(2):
-                collect(scopy if jp else vcopy, key, key + (jp,), jp)
-            quantize(key, E5M2 if key[0] == "s" else E4M3)
-        for q in range(4):
-            cosi(0, q)
-
-        def units(i):
-            return [(i % 2, 4 * (i // 2) + j) for j in range(4)]
-
-        def unit(i, j):
-            h, q = units(i)[j]
-            for g in range(3):
-                matmul(h, q, g)
-            expo(h, q)
-            cosi(h, q)
-            side(i, j)
-
-        def give_back(i):
-            for u in units(i):
-                back(*u)
-            for u in units(i):
-                finish(*u)
+            exponential(1, q)
+        for g in range(PASSES):
+            quantize(("dirs", 1, g))
+        for q in (0, 1, 3):
+            times_cosine_gpsimd(1, q)
 
         for q in range(4):
-            matmul(1, q, 0)
-        give_back(0)
-        store(0, 0, 0, 512)
-        for g in (1, 2):
-            for q in range(4):
-                matmul(1, q, g)
-        for q in range(4):
-            expo(1, q)
-            cosi(1, q)
-            side(1, q)
-        side(1, 4)
+            times_light(0, q)
+        store(0, 0, 0, W)
+        times_cosine_vector(1, 2)
+        interleave_vector(2, 1)
+        interleave_vector(2, 0)
+
+        def unit(h, q):
+            for g in range(PASSES):
+                multiply(h, q, g)
+            exponential(h, q)
+
+        side = {
+            2: ((), ((interleave_scalar, 2, 0), (interleave_scalar, 2, 1), (interleave_scalar, 2, 2), (interleave_vector, 2, 2), (0, 2, 0), (0, 2, 1), (0, 2, 2))),
+            3: ((), ((interleave_scalar, 3, 0), (interleave_vector, 3, 1), (interleave_vector, 3, 0), (interleave_vector, 3, 2))),
+            4: ((), ((interleave_scalar, 3, 2), (interleave_scalar, 3, 1), (0, 3, 0), (0, 3, 2), (0, 3, 1))),
+        }
         for i in range(2, 7):
+            h, b = RUNS[i]
+            ph, pb = RUNS[i - 1]
+            q0, pq0 = 4 * b, 4 * pb
             for j in range(4):
-                unit(i, j)
-            give_back(i - 1)
-            store((i - 1) % 2, (i - 1) // 2, 0, 512)
-            side(i, 4)
-        unit(7, 0)
-        unit(7, 1)
-        give_back(6)
-        store(0, 3, 0, 512)
-        unit(7, 2)
-        unit(7, 3)
-        for j in range(4):
-            back(*units(7)[j])
-            finish(*units(7)[j])
-            if j == 1:
-                store(1, 3, 0, 256)
-            elif j > 1:
-                store(1, 3, 128 * j, 128 * j + 128)
+                unit(h, q0 + j)
+                if j != 2:
+                    times_cosine_gpsimd(h, q0 + j)
+            for j in range(4):
+                turn_back(ph, pq0 + j)
+            for j in range(4):
+                if j == 3:
+                    times_cosine_vector(h, q0 + 2)
+                times_light(ph, pq0 + j)
+            store(ph, pb, 0, W)
+            for fn, sb, g in side.get(i, ((), ()))[1]:
+                if fn == 0:
+                    quantize(("dirs", sb, g))
+                else:
+                    fn(sb, g)
+
+        unit(1, 12)
+        turn_back(0, 12)
+        turn_back(0, 13)
+        times_light(0, 12)
+        times_light(0, 13)
+        times_cosine_gpsimd(1, 12)
+        unit(1, 13)
+        turn_back(0, 14)
+        turn_back(0, 15)
+        times_light(0, 14)
+        times_cosine_vector(1, 13)
+        times_light(0, 15)
+        store(0, 3, 0, W)
+        unit(1, 14)
+        turn_back(1, 12)
+        turn_back(1, 13)
+        times_light(1, 12)
+        times_cosine_vector(1, 14)
+        times_light(1, 13)
+        store(1, 3, 0, 256)
+        unit(1, 15)
+        turn_back(1, 14)
+        times_cosine_vector(1, 15)
+        times_light(1, 14)
+        turn_back(1, 15)
+        times_light(1, 15)
+        store(1, 3, 256, W)

@@ -17,15 +17,25 @@ MULT = mybir.AluOpType.mult
 ADD = mybir.AluOpType.add
 
 P = 128
-J = 4
-W = 512
+PACK = 4
+K_PASS = P * PACK
+COLS = 512
+TILES = COLS // P
 
-SPECULAR = 2
 PASSES = 3
+SPECULAR = 2
 
 RUNS = [(0, 0), (1, 0), (0, 1), (1, 1), (0, 2), (1, 2), (0, 3), (1, 3)]
+LAST_HALF, LAST_BLOCK = RUNS[-1]
 
-VECTOR_COLUMNS = [(336, 336, 336), (192, 320, 320), (192, 320, 192), (96, 256, 192)]
+VECTOR_COLUMNS = [(336, 336, 336), (320, 224, 288), (128, 320, 224), (192, 352, 128)]
+
+PREPARE = {
+    1: [("V", 2, 1), ("V", 2, 0)],
+    2: [("S", 2, 0), ("S", 2, 1), ("S", 2, 2), ("V", 2, 2), ("Q", 2, 0), ("Q", 2, 1), ("Q", 2, 2)],
+    3: [("S", 3, 0), ("V", 3, 1), ("V", 3, 0), ("V", 3, 2)],
+    4: [("S", 3, 2), ("S", 3, 1), ("Q", 3, 0), ("Q", 3, 2), ("Q", 3, 1)],
+}
 
 
 def tile_log_brdf_light_s2_kernel(tc, coef, basis, spec, spec_basis, mean_log, cosine, light, out):
@@ -35,7 +45,7 @@ def tile_log_brdf_light_s2_kernel(tc, coef, basis, spec, spec_basis, mean_log, c
     with ExitStack() as ctx:
         keep = ctx.enter_context(tc.tile_pool(name="keep", bufs=1))
         grouped_pool = ctx.enter_context(tc.tile_pool(name="grouped", bufs=4))
-        exp_pool = ctx.enter_context(tc.tile_pool(name="exp", bufs=8))
+        exp_pool = ctx.enter_context(tc.tile_pool(name="exp", bufs=2 * TILES))
         out_pool = ctx.enter_context(tc.tile_pool(name="out", bufs=4))
         psum = ctx.enter_context(tc.psum_pool(name="psum", bufs=4))
         ctx.enter_context(tc.manual_schedule())
@@ -44,75 +54,77 @@ def tile_log_brdf_light_s2_kernel(tc, coef, basis, spec, spec_basis, mean_log, c
             return keep.tile(shape, dtype, name=name, align_bytes=64)
 
         def by_four(rows):
-            return rows.rearrange("(p j) w -> p j w", j=J)
+            return rows.rearrange("(p j) w -> p j w", j=PACK)
+
+        def half_rows(matrix, h):
+            return matrix[h * COLS : (h + 1) * COLS, :]
 
         points, dirs, light_in = {}, {}, {}
 
         def load_coef(h, k0, k1):
-            t = fixed([P, J, k1 - k0], BF16, "coef_%d_%d" % (h, k0))
-            nc.sync.dma_start(out=t[:], in_=by_four(coef[h * W : (h + 1) * W, k0:k1]))
-            for g in range(k0 // W, k1 // W):
-                points[h, g] = t[:, :, g * W - k0 : (g + 1) * W - k0]
+            t = fixed([P, PACK, k1 - k0], BF16, "coef_%d_%d" % (h, k0))
+            nc.sync.dma_start(out=t[:], in_=by_four(half_rows(coef, h)[:, k0:k1]))
+            for g in range(k0 // K_PASS, k1 // K_PASS):
+                points[h, g] = t[:, :, g * K_PASS - k0 : (g + 1) * K_PASS - k0]
 
         def load_spec(h):
-            t = fixed([P, J, R], BF16, "spec_%d" % h)
-            nc.sync.dma_start(out=t[:], in_=by_four(spec[h * W : (h + 1) * W, :]))
+            t = fixed([P, PACK, R], BF16, "spec_%d" % h)
+            nc.sync.dma_start(out=t[:], in_=by_four(half_rows(spec, h)))
             points[h, SPECULAR] = t[:]
 
         def load_dirs(g, n0, n1):
-            t = fixed([P, J, n1 - n0], BF16, "dirs_%d_%d" % (g, n0))
-            rows = spec_basis if g == SPECULAR else basis[g * W : (g + 1) * W, :]
+            t = fixed([P, PACK, n1 - n0], BF16, "dirs_%d_%d" % (g, n0))
+            rows = spec_basis if g == SPECULAR else basis[g * K_PASS : (g + 1) * K_PASS, :]
             nc.sync.dma_start(out=t[:], in_=by_four(rows[:, n0:n1]))
-            for b in range(n0 // W, n1 // W):
-                dirs[b, g] = t[:, :, b * W - n0 : (b + 1) * W - n0]
+            for b in range(n0 // COLS, n1 // COLS):
+                dirs[b, g] = t[:, :, b * COLS - n0 : (b + 1) * COLS - n0]
 
         def load_light(h, n0, n1):
-            t = fixed([P, J, n1 - n0], BF16, "light_%d_%d" % (h, n0))
-            nc.sync.dma_start(out=t[:], in_=by_four(light[h * W : (h + 1) * W, n0:n1]))
-            for q in range(n0 // P, n1 // P):
-                light_in[h, q] = t[:, :, q * P - n0 : (q + 1) * P - n0]
+            t = fixed([P, PACK, n1 - n0], BF16, "light_%d_%d" % (h, n0))
+            nc.sync.dma_start(out=t[:], in_=by_four(half_rows(light, h)[:, n0:n1]))
+            for b in range(n0 // COLS, n1 // COLS):
+                light_in[h, b] = t[:, :, b * COLS - n0 : (b + 1) * COLS - n0]
 
         vectors = fixed([P, P], BF16, "vectors")
         nc.vector.memset(vectors[:], 0.0)
 
-        load_coef(0, 0, W)
-        load_dirs(0, 0, W)
+        load_coef(0, 0, K_PASS)
         nc.sync.dma_start(out=vectors[0:16, :], in_=mean_log.rearrange("(t p) -> t p", p=P))
         nc.sync.dma_start(out=vectors[16:32, :], in_=cosine.rearrange("(t p) -> t p", p=P))
-        load_coef(0, W, K)
-        load_dirs(1, 0, W)
+        load_dirs(0, 0, COLS)
+        load_coef(0, K_PASS, K)
+        load_dirs(1, 0, COLS)
         load_spec(0)
-        load_dirs(SPECULAR, 0, W)
+        load_dirs(SPECULAR, 0, COLS)
         load_coef(1, 0, K)
         load_spec(1)
-        load_light(0, 0, W)
+        load_light(0, 0, COLS)
         for g in range(PASSES):
-            load_dirs(g, W, 2 * W)
-        load_light(1, 0, W)
+            load_dirs(g, COLS, 2 * COLS)
+        load_light(1, 0, COLS)
         for g in range(PASSES):
-            load_dirs(g, 2 * W, N)
-        load_light(0, W, N)
-        load_light(1, W, N)
+            load_dirs(g, 2 * COLS, N)
+        load_light(0, COLS, N)
+        load_light(1, COLS, N)
 
-        grouped, codes, scales, banks, split = {}, {}, {}, {}, {}
+        grouped, codes, scales, banks, sorted_words = {}, {}, {}, {}, {}
+
+        def code_type(key):
+            return E5M2 if key[0] == "points" and key[2] == SPECULAR else E4M3
 
         def group(key):
             if key not in grouped:
-                grouped[key] = grouped_pool.tile([P, W, J], BF16, name="grouped", align_bytes=64)
+                grouped[key] = grouped_pool.tile([P, COLS, PACK], BF16, name="grouped", align_bytes=64)
             return grouped[key]
 
         def quantize(key):
-            name = "%s_%d_%d" % key
-            codes[key] = fixed([P, W], U32, "codes_" + name)
-            scales[key] = fixed([P, W], U8, "scales_" + name)
+            codes[key] = fixed([P, COLS], U32, "codes_%s_%d_%d" % key)
+            scales[key] = fixed([P, COLS], U8, "scales_%s_%d_%d" % key)
             nc.vector.quantize_mx(
                 out=codes[key][:].bitcast(code_type(key)),
                 scales=scales[key][:],
                 in_=group(key)[:].rearrange("p n t -> p (n t)"),
             )
-
-        def code_type(key):
-            return E5M2 if key[0] == "points" and key[2] == SPECULAR else E4M3
 
         def interleave(engine_copy, b, g, n0, n1):
             engine_copy(
@@ -124,156 +136,207 @@ def tile_log_brdf_light_s2_kernel(tc, coef, basis, spec, spec_basis, mean_log, c
             interleave(vector_copy, b, g, 0, VECTOR_COLUMNS[b][g])
 
         def interleave_scalar(b, g):
-            interleave(scalar_copy, b, g, VECTOR_COLUMNS[b][g], W)
+            interleave(scalar_copy, b, g, VECTOR_COLUMNS[b][g], COLS)
 
         def words(h, g):
             return points[h, g].bitcast(F32)
 
-        def split_words(engine_copy, h, g):
-            split[h, g] = fixed([P, J, 2, P], F32, "split_%d_%d" % (h, g))
-            engine_copy(out=split[h, g][:], in_=words(h, g).rearrange("p j (q u) -> p j u q", u=2))
+        def sort_words(engine_copy, h, g):
+            sorted_words[h, g] = fixed([P, PACK, 2, P], F32, "sorted_%d_%d" % (h, g))
+            engine_copy(out=sorted_words[h, g][:], in_=words(h, g).rearrange("p j (q u) -> p j u q", u=2))
 
         def turn(h, g):
-            for half in range(2):
-                bank = psum.tile([P, W], F32, name="turned")
-                for j in range(2):
+            for pair in range(2):
+                bank = psum.tile([P, COLS], F32, name="turned")
+                for i in range(2):
                     for u in range(2):
-                        row = 2 * half + j
-                        if (h, g) in split:
-                            source = split[h, g][:, row, u, :]
+                        j = 2 * pair + i
+                        if (h, g) in sorted_words:
+                            source = sorted_words[h, g][:, j, u, :]
                         else:
-                            source = words(h, g)[:, row, u::2]
-                        spot = (2 * j + u) * P
+                            source = words(h, g)[:, j, u::2]
+                        spot = (2 * i + u) * P
                         nc.tensor.transpose(bank[:, spot : spot + P], source, ident[:])
-                banks["points", h, g, half] = bank
+                banks["points", h, g, pair] = bank
 
-        def gather(engine_copy, h, g, half):
+        def gather(engine_copy, h, g, pair):
             engine_copy(
                 out=group(("points", h, g))[:]
                 .rearrange("p n t -> p (n t)")
-                .bitcast(F32)[:, half * W : (half + 1) * W]
-                .rearrange("p (j r u) -> p j r u", j=2, u=2),
-                in_=banks["points", h, g, half][:].rearrange("p (j u r) -> p j r u", j=2, u=2),
+                .bitcast(F32)[:, pair * COLS : (pair + 1) * COLS]
+                .rearrange("p (i r u) -> p i r u", i=2, u=2),
+                in_=banks["points", h, g, pair][:].rearrange("p (i u r) -> p i r u", i=2, u=2),
             )
 
         acc, e, outs = {}, {}, {}
 
-        def multiply(h, q, g):
-            if g == 0:
-                acc[h, q] = psum.tile([P, W], F32, name="acc")
-            d, p = ("dirs", q // 4, g), ("points", h, g)
-            c = (q % 4) * P
+        def tiles_of(b):
+            return range(TILES * b, TILES * (b + 1))
+
+        def multiply(bank, stationary, moving, c, g):
             nc.tensor.matmul_mx(
-                out=acc[h, q][:],
-                lhsT=codes[d][:, c : c + P].bitcast(code_type(d)),
-                lhsT_scale=scales[d][:, c : c + P],
-                rhs=codes[p][:].bitcast(code_type(p)),
-                rhs_scale=scales[p][:],
+                out=bank[:],
+                lhsT=codes[stationary][:, c : c + P].bitcast(code_type(stationary)),
+                lhsT_scale=scales[stationary][:, c : c + P],
+                rhs=codes[moving][:].bitcast(code_type(moving)),
+                rhs_scale=scales[moving][:],
                 start=(g == 0),
                 stop=(g == PASSES - 1),
             )
 
+        def unit_pass(h, q, g):
+            if g == 0:
+                acc[h, q] = psum.tile([P, COLS], F32, name="acc")
+            multiply(acc[h, q], ("dirs", q // TILES, g), ("points", h, g), (q % TILES) * P, g)
+
+        def run_pass(h, b, g):
+            for q in tiles_of(b):
+                unit_pass(h, q, g)
+
         def exponential(h, q):
-            e[h, q] = exp_pool.tile([P, W], F32, name="e")
+            e[h, q] = exp_pool.tile([P, COLS], F32, name="e")
             nc.scalar.activation(out=e[h, q][:], in_=acc[h, q][:], func=EXP, bias=columns[:, q : q + 1])
+
+        def cosine_column(q):
+            return columns[:, 16 + q : 17 + q]
 
         def times_cosine_gpsimd(h, q):
             nc.gpsimd.tensor_scalar(
-                out=e[h, q][:], in0=e[h, q][:], scalar1=columns[:, 16 + q : 17 + q], scalar2=0.0, op0=MULT, op1=ADD
+                out=e[h, q][:], in0=e[h, q][:], scalar1=cosine_column(q), scalar2=0.0, op0=MULT, op1=ADD
             )
 
         def times_cosine_vector(h, q):
             nc.vector.tensor_scalar(
-                out=e[h, q][:], in0=e[h, q][:], scalar1=columns[:, 16 + q : 17 + q], scalar2=None, op0=MULT
+                out=e[h, q][:], in0=e[h, q][:], scalar1=cosine_column(q), scalar2=None, op0=MULT
             )
 
+        def result(h, b):
+            if (h, b) not in outs:
+                outs[h, b] = out_pool.tile([P, PACK, COLS], F32, name="o")
+            return outs[h, b]
+
         def turn_back(h, q):
-            bank = psum.tile([P, W], F32, name="turned")
-            for j in range(J):
+            bank = psum.tile([P, COLS], F32, name="turned")
+            for j in range(PACK):
                 nc.tensor.transpose(bank[:, j * P : (j + 1) * P], e[h, q][:, j * P : (j + 1) * P], ident[:])
-            banks["out", h, q] = bank
+            banks["unit", h, q] = bank
 
         def times_light(h, q):
-            b, c = q // 4, (q % 4) * P
-            if (h, b) not in outs:
-                outs[h, b] = out_pool.tile([P, J, W], F32, name="o")
+            b, c = q // TILES, (q % TILES) * P
             nc.vector.tensor_tensor(
-                out=outs[h, b][:, :, c : c + P],
-                in0=banks["out", h, q][:].rearrange("p (j n) -> p j n", j=J),
-                in1=light_in[h, q],
+                out=result(h, b)[:, :, c : c + P],
+                in0=banks["unit", h, q][:].rearrange("p (j n) -> p j n", j=PACK),
+                in1=light_in[h, b][:, :, c : c + P],
                 op=MULT,
             )
 
-        def store(h, b, c0, c1):
-            rows = out[h * W : (h + 1) * W, b * W + c0 : b * W + c1]
-            nc.sync.dma_start(out=by_four(rows), in_=outs[h, b][:, :, c0:c1])
+        def turn_back_row(h, b, j):
+            bank = psum.tile([P, COLS], F32, name="turned")
+            for i, q in enumerate(tiles_of(b)):
+                nc.tensor.transpose(bank[:, i * P : (i + 1) * P], e[h, q][:, j * P : (j + 1) * P], ident[:])
+            banks["row", h, b, j] = bank
+
+        def times_light_row(h, b, j):
+            nc.vector.tensor_tensor(
+                out=result(h, b)[:, j, :], in0=banks["row", h, b, j][:], in1=light_in[h, b][:, j, :], op=MULT
+            )
+
+        def store_rows(h, b, j0, j1):
+            rows = by_four(half_rows(out, h)[:, b * COLS : (b + 1) * COLS])
+            nc.sync.dma_start(out=rows[:, j0:j1, :], in_=outs[h, b][:, j0:j1, :])
+
+        light_cosine = {}
+
+        def make_light_cosine(engine, j):
+            if j % 2 == 0:
+                two_rows = grouped_pool.tile([P, 2, COLS], F32, name="grouped", align_bytes=64)
+                light_cosine[j], light_cosine[j + 1] = two_rows[:, 0, :], two_rows[:, 1, :]
+            engine.tensor_tensor(
+                out=light_cosine[j], in0=light_in[LAST_HALF, LAST_BLOCK][:, j, :], in1=cosine_row[:], op=MULT
+            )
+
+        def last_unit(j):
+            acc["last", j] = psum.tile([P, COLS], F32, name="acc")
+            for g in range(PASSES):
+                multiply(acc["last", j], ("points", LAST_HALF, g), ("dirs", LAST_BLOCK, g), j * P, g)
+
+        def last_exponential(j):
+            t = exp_pool.tile([P, COLS], F32, name="e")
+            nc.vector.tensor_tensor(out=t[:], in0=acc["last", j][:], in1=mean_row[:], op=ADD)
+            nc.scalar.activation(out=t[:], in_=t[:], func=EXP)
+            e["last", j] = t
+
+        def finish_last(engine, j):
+            engine.tensor_tensor(
+                out=result(LAST_HALF, LAST_BLOCK)[:, j, :], in0=e["last", j][:], in1=light_cosine[j], op=MULT
+            )
+            store_rows(LAST_HALF, LAST_BLOCK, j, j + 1)
 
         ident = fixed([P, P], F32, "ident")
         make_identity(nc, ident[:])
         columns = fixed([P, 32], F32, "columns")
+        mean_row = fixed([P, COLS], F32, "mean_row")
+        cosine_row = fixed([P, COLS], F32, "cosine_row")
+
         first = fixed([P, 8], F32, "first")
         nc.vector.memset(first[:], 0.0)
         nc.scalar.activation(out=first[:], in_=first[:], func=EXP)
-        idle = ("idle", 0, 0)
-        nc.vector.memset(group(idle)[:], 0.0)
-        quantize(idle)
 
-        def keep_clock(n):
-            bank = psum.tile([P, W], F32, name="turned")
-            for i in range(n):
-                nc.tensor.matmul_mx(
-                    out=bank[:],
-                    lhsT=codes[idle][:, 0:P].bitcast(E4M3),
-                    lhsT_scale=scales[idle][:, 0:P],
-                    rhs=codes[idle][:].bitcast(E4M3),
-                    rhs_scale=scales[idle][:],
-                    start=(i == 0),
-                    stop=(i == n - 1),
-                )
+        zeros = ("zeros", 0, 0)
+        nc.vector.memset(group(zeros)[:], 0.0)
+        quantize(zeros)
 
-        def pass_of_run(h, b, g):
-            for q in range(4 * b, 4 * b + 4):
-                multiply(h, q, g)
+        def spread(name, t):
+            bank = psum.tile([P, COLS], F32, name="turned")
+            for i in range(TILES):
+                column = columns[:, t + i : t + i + 1].to_broadcast([P, P])
+                nc.tensor.transpose(bank[:, i * P : (i + 1) * P], column, ident[:])
+            banks[name] = bank
 
+        vectors_f32 = fixed([P, P], F32, "vectors_f32")
+        vector_copy(out=vectors_f32[:], in_=vectors[:])
         turn(0, 0)
         gather(scalar_copy, 0, 0, 0)
         gather(scalar_copy, 0, 0, 1)
+        vectors_bank = psum.tile([P, COLS], F32, name="turned")
+        nc.tensor.transpose(vectors_bank[:, 0:P], vectors_f32[:], ident[:])
+        vector_copy(out=columns[:], in_=vectors_bank[:, 0:32])
+        spread("mean", TILES * LAST_BLOCK)
+        spread("cosine", 16 + TILES * LAST_BLOCK)
         interleave_vector(0, 0)
         interleave_scalar(0, 0)
+        scalar_copy(out=mean_row[:], in_=banks["mean"][:])
         quantize(("points", 0, 0))
         turn(0, 1)
-        wide = fixed([P, P], F32, "wide")
-        nc.vector.tensor_copy(out=wide[:], in_=vectors[:])
         quantize(("dirs", 0, 0))
-        columns_bank = psum.tile([P, W], F32, name="turned")
-        nc.tensor.transpose(columns_bank[:, 0:P], wide[:], ident[:])
+        vector_copy(out=cosine_row[:], in_=banks["cosine"][:])
         gather(scalar_copy, 0, 1, 0)
         gather(scalar_copy, 0, 1, 1)
-        pass_of_run(0, 0, 0)
+        run_pass(0, 0, 0)
         interleave_vector(0, 1)
         interleave_scalar(0, 1)
         quantize(("points", 0, 1))
-        nc.vector.tensor_copy(out=columns[:], in_=columns_bank[:, 0:32])
         quantize(("dirs", 0, 1))
         turn(0, SPECULAR)
-        pass_of_run(0, 0, 1)
+        run_pass(0, 0, 1)
         interleave_vector(0, SPECULAR)
         interleave_scalar(0, SPECULAR)
         gather(vector_copy, 0, SPECULAR, 1)
         gather(scalar_copy, 0, SPECULAR, 0)
         quantize(("dirs", 0, SPECULAR))
         quantize(("points", 0, SPECULAR))
-        split_words(scalar_copy, 1, 1)
+
+        sort_words(scalar_copy, 1, 1)
         turn(1, 0)
-        pass_of_run(0, 0, SPECULAR)
+        run_pass(0, 0, SPECULAR)
         gather(vector_copy, 1, 0, 0)
         gather(scalar_copy, 1, 0, 1)
-        split_words(vector_copy, 1, SPECULAR)
+        sort_words(vector_copy, 1, SPECULAR)
         turn(1, 1)
-        for q in range(4):
+        for q in tiles_of(0):
             exponential(0, q)
         quantize(("points", 1, 0))
-        pass_of_run(1, 0, 0)
+        run_pass(1, 0, 0)
         gather(vector_copy, 1, 1, 0)
         gather(scalar_copy, 1, 1, 1)
         turn(1, SPECULAR)
@@ -286,85 +349,83 @@ def tile_log_brdf_light_s2_kernel(tc, coef, basis, spec, spec_basis, mean_log, c
         quantize(("points", 1, 1))
         gather(vector_copy, 1, SPECULAR, 0)
         gather(scalar_copy, 1, SPECULAR, 1)
-        keep_clock(2)
-        for q in range(4):
+        zeros_bank = psum.tile([P, COLS], F32, name="turned")
+        for i in range(2):
+            nc.tensor.matmul_mx(
+                out=zeros_bank[:],
+                lhsT=codes[zeros][:, 0:P].bitcast(E4M3),
+                lhsT_scale=scales[zeros][:, 0:P],
+                rhs=codes[zeros][:].bitcast(E4M3),
+                rhs_scale=scales[zeros][:],
+                start=(i == 0),
+                stop=(i == 1),
+            )
+        for q in tiles_of(0):
             turn_back(0, q)
-        pass_of_run(1, 0, 1)
+        run_pass(1, 0, 1)
         interleave_vector(1, 1)
         interleave_scalar(1, 1)
         quantize(("points", 1, SPECULAR))
         interleave_vector(1, SPECULAR)
         interleave_scalar(1, SPECULAR)
-        pass_of_run(1, 0, SPECULAR)
-        for q in range(4):
+        run_pass(1, 0, SPECULAR)
+        for q in tiles_of(0):
             exponential(1, q)
         for g in range(PASSES):
             quantize(("dirs", 1, g))
         for q in (0, 1, 3):
             times_cosine_gpsimd(1, q)
-
-        for q in range(4):
+        for q in tiles_of(0):
             times_light(0, q)
-        store(0, 0, 0, W)
+        store_rows(0, 0, 0, PACK)
         times_cosine_vector(1, 2)
-        interleave_vector(2, 1)
-        interleave_vector(2, 0)
 
-        def unit(h, q):
-            for g in range(PASSES):
-                multiply(h, q, g)
-            exponential(h, q)
-
-        side = {
-            2: ((), ((interleave_scalar, 2, 0), (interleave_scalar, 2, 1), (interleave_scalar, 2, 2), (interleave_vector, 2, 2), (0, 2, 0), (0, 2, 1), (0, 2, 2))),
-            3: ((), ((interleave_scalar, 3, 0), (interleave_vector, 3, 1), (interleave_vector, 3, 0), (interleave_vector, 3, 2))),
-            4: ((), ((interleave_scalar, 3, 2), (interleave_scalar, 3, 1), (0, 3, 0), (0, 3, 2), (0, 3, 1))),
-        }
-        for i in range(2, 7):
-            h, b = RUNS[i]
-            ph, pb = RUNS[i - 1]
-            q0, pq0 = 4 * b, 4 * pb
-            for j in range(4):
-                unit(h, q0 + j)
-                if j != 2:
-                    times_cosine_gpsimd(h, q0 + j)
-            for j in range(4):
-                turn_back(ph, pq0 + j)
-            for j in range(4):
-                if j == 3:
-                    times_cosine_vector(h, q0 + 2)
-                times_light(ph, pq0 + j)
-            store(ph, pb, 0, W)
-            for fn, sb, g in side.get(i, ((), ()))[1]:
-                if fn == 0:
-                    quantize(("dirs", sb, g))
+        def prepare(i):
+            for what, b, g in PREPARE.get(i, []):
+                if what == "V":
+                    interleave_vector(b, g)
+                elif what == "S":
+                    interleave_scalar(b, g)
                 else:
-                    fn(sb, g)
+                    quantize(("dirs", b, g))
 
-        unit(1, 12)
-        turn_back(0, 12)
-        turn_back(0, 13)
-        times_light(0, 12)
-        times_light(0, 13)
-        times_cosine_gpsimd(1, 12)
-        unit(1, 13)
-        turn_back(0, 14)
-        turn_back(0, 15)
-        times_light(0, 14)
-        times_cosine_vector(1, 13)
-        times_light(0, 15)
-        store(0, 3, 0, W)
-        unit(1, 14)
-        turn_back(1, 12)
-        turn_back(1, 13)
-        times_light(1, 12)
-        times_cosine_vector(1, 14)
-        times_light(1, 13)
-        store(1, 3, 0, 256)
-        unit(1, 15)
-        turn_back(1, 14)
-        times_cosine_vector(1, 15)
-        times_light(1, 14)
-        turn_back(1, 15)
-        times_light(1, 15)
-        store(1, 3, 256, W)
+        prepare(1)
+        for i in range(2, len(RUNS) - 1):
+            h, b = RUNS[i]
+            for q in tiles_of(b):
+                for g in range(PASSES):
+                    unit_pass(h, q, g)
+                exponential(h, q)
+                times_cosine_gpsimd(h, q)
+            h_before, b_before = RUNS[i - 1]
+            for q in tiles_of(b_before):
+                turn_back(h_before, q)
+            if i == len(RUNS) - 2:
+                for j in range(PACK):
+                    make_light_cosine(nc.gpsimd if j == PACK - 1 else nc.vector, j)
+            for q in tiles_of(b_before):
+                times_light(h_before, q)
+            store_rows(h_before, b_before, 0, PACK)
+            prepare(i)
+
+        h, b = RUNS[-2]
+        last_unit(0)
+        last_unit(1)
+        for j in range(PACK):
+            turn_back_row(h, b, j)
+        last_unit(2)
+        last_unit(3)
+        last_exponential(0)
+        last_exponential(1)
+        times_light_row(h, b, 0)
+        times_light_row(h, b, 1)
+        store_rows(h, b, 0, 2)
+        finish_last(nc.gpsimd, 0)
+        finish_last(nc.gpsimd, 1)
+        times_light_row(h, b, 2)
+        last_exponential(2)
+        times_light_row(h, b, 3)
+        store_rows(h, b, 2, 4)
+        last_exponential(3)
+        finish_last(nc.vector, 2)
+        finish_last(nc.vector, 3)

from contextlib import ExitStack

import concourse.mybir as mybir
from concourse.masks import make_identity

M, K, R, N = 1024, 1024, 512, 2048
FLOPS = 2 * M * (K + R) * N

F32 = mybir.dt.float32
BF16 = mybir.dt.bfloat16
U32 = mybir.dt.uint32
U8 = mybir.dt.uint8
E4M3 = mybir.dt.float8_e4m3fn_x4
E5M2 = mybir.dt.float8_e5m2_x4
EXP = mybir.ActivationFunctionType.Exp
MULT = mybir.AluOpType.mult
ADD = mybir.AluOpType.add

P = 128
PACK = 4
K_PASS = P * PACK
COLS = 512
TILES = COLS // P

PASSES = 3
SPECULAR = 2

RUNS = [(0, 0), (1, 0), (0, 1), (1, 1), (0, 2), (1, 2), (0, 3), (1, 3)]
LAST_HALF, LAST_BLOCK = RUNS[-1]

VECTOR_COLUMNS = [(336, 336, 336), (320, 224, 288), (128, 320, 224), (192, 352, 128)]

PREPARE = {
    1: [("V", 2, 1), ("V", 2, 0)],
    2: [("S", 2, 0), ("S", 2, 1), ("S", 2, 2), ("V", 2, 2), ("Q", 2, 0), ("Q", 2, 1), ("Q", 2, 2)],
    3: [("S", 3, 0), ("V", 3, 1), ("V", 3, 0), ("V", 3, 2)],
    4: [("S", 3, 2), ("S", 3, 1), ("Q", 3, 0), ("Q", 3, 2), ("Q", 3, 1)],
}


def tile_log_brdf_light_s2_kernel(tc, coef, basis, spec, spec_basis, mean_log, cosine, light, out):
    nc = tc.nc
    vector_copy, scalar_copy = nc.vector.tensor_copy, nc.scalar.copy

    with ExitStack() as ctx:
        keep = ctx.enter_context(tc.tile_pool(name="keep", bufs=1))
        grouped_pool = ctx.enter_context(tc.tile_pool(name="grouped", bufs=4))
        exp_pool = ctx.enter_context(tc.tile_pool(name="exp", bufs=2 * TILES))
        out_pool = ctx.enter_context(tc.tile_pool(name="out", bufs=4))
        psum = ctx.enter_context(tc.psum_pool(name="psum", bufs=4))
        ctx.enter_context(tc.manual_schedule())

        def fixed(shape, dtype, name):
            return keep.tile(shape, dtype, name=name, align_bytes=64)

        def by_four(rows):
            return rows.rearrange("(p j) w -> p j w", j=PACK)

        def half_rows(matrix, h):
            return matrix[h * COLS : (h + 1) * COLS, :]

        points, dirs, light_in = {}, {}, {}

        def load_coef(h, k0, k1):
            t = fixed([P, PACK, k1 - k0], BF16, "coef_%d_%d" % (h, k0))
            nc.sync.dma_start(out=t[:], in_=by_four(half_rows(coef, h)[:, k0:k1]))
            for g in range(k0 // K_PASS, k1 // K_PASS):
                points[h, g] = t[:, :, g * K_PASS - k0 : (g + 1) * K_PASS - k0]

        def load_spec(h):
            t = fixed([P, PACK, R], BF16, "spec_%d" % h)
            nc.sync.dma_start(out=t[:], in_=by_four(half_rows(spec, h)))
            points[h, SPECULAR] = t[:]

        def load_dirs(g, n0, n1):
            t = fixed([P, PACK, n1 - n0], BF16, "dirs_%d_%d" % (g, n0))
            rows = spec_basis if g == SPECULAR else basis[g * K_PASS : (g + 1) * K_PASS, :]
            nc.sync.dma_start(out=t[:], in_=by_four(rows[:, n0:n1]))
            for b in range(n0 // COLS, n1 // COLS):
                dirs[b, g] = t[:, :, b * COLS - n0 : (b + 1) * COLS - n0]

        def load_light(h, n0, n1):
            t = fixed([P, PACK, n1 - n0], BF16, "light_%d_%d" % (h, n0))
            nc.sync.dma_start(out=t[:], in_=by_four(half_rows(light, h)[:, n0:n1]))
            for b in range(n0 // COLS, n1 // COLS):
                light_in[h, b] = t[:, :, b * COLS - n0 : (b + 1) * COLS - n0]

        vectors = fixed([P, P], BF16, "vectors")
        nc.vector.memset(vectors[:], 0.0)

        load_coef(0, 0, K_PASS)
        nc.sync.dma_start(out=vectors[0:16, :], in_=mean_log.rearrange("(t p) -> t p", p=P))
        nc.sync.dma_start(out=vectors[16:32, :], in_=cosine.rearrange("(t p) -> t p", p=P))
        load_dirs(0, 0, COLS)
        load_coef(0, K_PASS, K)
        load_dirs(1, 0, COLS)
        load_spec(0)
        load_dirs(SPECULAR, 0, COLS)
        load_coef(1, 0, K)
        load_spec(1)
        load_light(0, 0, COLS)
        for g in range(PASSES):
            load_dirs(g, COLS, 2 * COLS)
        load_light(1, 0, COLS)
        for g in range(PASSES):
            load_dirs(g, 2 * COLS, N)
        load_light(0, COLS, N)
        load_light(1, COLS, N)

        grouped, codes, scales, banks, sorted_words = {}, {}, {}, {}, {}

        def code_type(key):
            return E5M2 if key[0] == "points" and key[2] == SPECULAR else E4M3

        def group(key):
            if key not in grouped:
                grouped[key] = grouped_pool.tile([P, COLS, PACK], BF16, name="grouped", align_bytes=64)
            return grouped[key]

        def quantize(key):
            codes[key] = fixed([P, COLS], U32, "codes_%s_%d_%d" % key)
            scales[key] = fixed([P, COLS], U8, "scales_%s_%d_%d" % key)
            nc.vector.quantize_mx(
                out=codes[key][:].bitcast(code_type(key)),
                scales=scales[key][:],
                in_=group(key)[:].rearrange("p n t -> p (n t)"),
            )

        def interleave(engine_copy, b, g, n0, n1):
            engine_copy(
                out=group(("dirs", b, g))[:, n0:n1, :].rearrange("p (c i) t -> p c t i", i=4),
                in_=dirs[b, g][:, :, n0:n1].rearrange("p t (c i) -> p c t i", i=4),
            )

        def interleave_vector(b, g):
            interleave(vector_copy, b, g, 0, VECTOR_COLUMNS[b][g])

        def interleave_scalar(b, g):
            interleave(scalar_copy, b, g, VECTOR_COLUMNS[b][g], COLS)

        def words(h, g):
            return points[h, g].bitcast(F32)

        def sort_words(engine_copy, h, g):
            sorted_words[h, g] = fixed([P, PACK, 2, P], F32, "sorted_%d_%d" % (h, g))
            engine_copy(out=sorted_words[h, g][:], in_=words(h, g).rearrange("p j (q u) -> p j u q", u=2))

        def turn(h, g):
            for pair in range(2):
                bank = psum.tile([P, COLS], F32, name="turned")
                for i in range(2):
                    for u in range(2):
                        j = 2 * pair + i
                        if (h, g) in sorted_words:
                            source = sorted_words[h, g][:, j, u, :]
                        else:
                            source = words(h, g)[:, j, u::2]
                        spot = (2 * i + u) * P
                        nc.tensor.transpose(bank[:, spot : spot + P], source, ident[:])
                banks["points", h, g, pair] = bank

        def gather(engine_copy, h, g, pair):
            engine_copy(
                out=group(("points", h, g))[:]
                .rearrange("p n t -> p (n t)")
                .bitcast(F32)[:, pair * COLS : (pair + 1) * COLS]
                .rearrange("p (i r u) -> p i r u", i=2, u=2),
                in_=banks["points", h, g, pair][:].rearrange("p (i u r) -> p i r u", i=2, u=2),
            )

        acc, e, outs = {}, {}, {}

        def tiles_of(b):
            return range(TILES * b, TILES * (b + 1))

        def multiply(bank, stationary, moving, c, g):
            nc.tensor.matmul_mx(
                out=bank[:],
                lhsT=codes[stationary][:, c : c + P].bitcast(code_type(stationary)),
                lhsT_scale=scales[stationary][:, c : c + P],
                rhs=codes[moving][:].bitcast(code_type(moving)),
                rhs_scale=scales[moving][:],
                start=(g == 0),
                stop=(g == PASSES - 1),
            )

        def unit_pass(h, q, g):
            if g == 0:
                acc[h, q] = psum.tile([P, COLS], F32, name="acc")
            multiply(acc[h, q], ("dirs", q // TILES, g), ("points", h, g), (q % TILES) * P, g)

        def run_pass(h, b, g):
            for q in tiles_of(b):
                unit_pass(h, q, g)

        def exponential(h, q):
            e[h, q] = exp_pool.tile([P, COLS], F32, name="e")
            nc.scalar.activation(out=e[h, q][:], in_=acc[h, q][:], func=EXP, bias=columns[:, q : q + 1])

        def cosine_column(q):
            return columns[:, 16 + q : 17 + q]

        def times_cosine_gpsimd(h, q):
            nc.gpsimd.tensor_scalar(
                out=e[h, q][:], in0=e[h, q][:], scalar1=cosine_column(q), scalar2=0.0, op0=MULT, op1=ADD
            )

        def times_cosine_vector(h, q):
            nc.vector.tensor_scalar(
                out=e[h, q][:], in0=e[h, q][:], scalar1=cosine_column(q), scalar2=None, op0=MULT
            )

        def result(h, b):
            if (h, b) not in outs:
                outs[h, b] = out_pool.tile([P, PACK, COLS], F32, name="o")
            return outs[h, b]

        def turn_back(h, q):
            bank = psum.tile([P, COLS], F32, name="turned")
            for j in range(PACK):
                nc.tensor.transpose(bank[:, j * P : (j + 1) * P], e[h, q][:, j * P : (j + 1) * P], ident[:])
            banks["unit", h, q] = bank

        def times_light(h, q):
            b, c = q // TILES, (q % TILES) * P
            nc.vector.tensor_tensor(
                out=result(h, b)[:, :, c : c + P],
                in0=banks["unit", h, q][:].rearrange("p (j n) -> p j n", j=PACK),
                in1=light_in[h, b][:, :, c : c + P],
                op=MULT,
            )

        def turn_back_row(h, b, j):
            bank = psum.tile([P, COLS], F32, name="turned")
            for i, q in enumerate(tiles_of(b)):
                nc.tensor.transpose(bank[:, i * P : (i + 1) * P], e[h, q][:, j * P : (j + 1) * P], ident[:])
            banks["row", h, b, j] = bank

        def times_light_row(h, b, j):
            nc.vector.tensor_tensor(
                out=result(h, b)[:, j, :], in0=banks["row", h, b, j][:], in1=light_in[h, b][:, j, :], op=MULT
            )

        def store_rows(h, b, j0, j1):
            rows = by_four(half_rows(out, h)[:, b * COLS : (b + 1) * COLS])
            nc.sync.dma_start(out=rows[:, j0:j1, :], in_=outs[h, b][:, j0:j1, :])

        light_cosine = {}

        def make_light_cosine(engine, j):
            if j % 2 == 0:
                two_rows = grouped_pool.tile([P, 2, COLS], F32, name="grouped", align_bytes=64)
                light_cosine[j], light_cosine[j + 1] = two_rows[:, 0, :], two_rows[:, 1, :]
            engine.tensor_tensor(
                out=light_cosine[j], in0=light_in[LAST_HALF, LAST_BLOCK][:, j, :], in1=cosine_row[:], op=MULT
            )

        def last_unit(j):
            acc["last", j] = psum.tile([P, COLS], F32, name="acc")
            for g in range(PASSES):
                multiply(acc["last", j], ("points", LAST_HALF, g), ("dirs", LAST_BLOCK, g), j * P, g)

        def last_exponential(j):
            t = exp_pool.tile([P, COLS], F32, name="e")
            nc.vector.tensor_tensor(out=t[:], in0=acc["last", j][:], in1=mean_row[:], op=ADD)
            nc.scalar.activation(out=t[:], in_=t[:], func=EXP)
            e["last", j] = t

        def finish_last(engine, j):
            engine.tensor_tensor(
                out=result(LAST_HALF, LAST_BLOCK)[:, j, :], in0=e["last", j][:], in1=light_cosine[j], op=MULT
            )
            store_rows(LAST_HALF, LAST_BLOCK, j, j + 1)

        ident = fixed([P, P], F32, "ident")
        make_identity(nc, ident[:])
        columns = fixed([P, 32], F32, "columns")
        mean_row = fixed([P, COLS], F32, "mean_row")
        cosine_row = fixed([P, COLS], F32, "cosine_row")

        first = fixed([P, 8], F32, "first")
        nc.vector.memset(first[:], 0.0)
        nc.scalar.activation(out=first[:], in_=first[:], func=EXP)

        zeros = ("zeros", 0, 0)
        nc.vector.memset(group(zeros)[:], 0.0)
        quantize(zeros)

        def spread(name, t):
            bank = psum.tile([P, COLS], F32, name="turned")
            for i in range(TILES):
                column = columns[:, t + i : t + i + 1].to_broadcast([P, P])
                nc.tensor.transpose(bank[:, i * P : (i + 1) * P], column, ident[:])
            banks[name] = bank

        vectors_f32 = fixed([P, P], F32, "vectors_f32")
        vector_copy(out=vectors_f32[:], in_=vectors[:])
        turn(0, 0)
        gather(scalar_copy, 0, 0, 0)
        gather(scalar_copy, 0, 0, 1)
        vectors_bank = psum.tile([P, COLS], F32, name="turned")
        nc.tensor.transpose(vectors_bank[:, 0:P], vectors_f32[:], ident[:])
        vector_copy(out=columns[:], in_=vectors_bank[:, 0:32])
        spread("mean", TILES * LAST_BLOCK)
        spread("cosine", 16 + TILES * LAST_BLOCK)
        interleave_vector(0, 0)
        interleave_scalar(0, 0)
        scalar_copy(out=mean_row[:], in_=banks["mean"][:])
        quantize(("points", 0, 0))
        turn(0, 1)
        quantize(("dirs", 0, 0))
        vector_copy(out=cosine_row[:], in_=banks["cosine"][:])
        gather(scalar_copy, 0, 1, 0)
        gather(scalar_copy, 0, 1, 1)
        run_pass(0, 0, 0)
        interleave_vector(0, 1)
        interleave_scalar(0, 1)
        quantize(("points", 0, 1))
        quantize(("dirs", 0, 1))
        turn(0, SPECULAR)
        run_pass(0, 0, 1)
        interleave_vector(0, SPECULAR)
        interleave_scalar(0, SPECULAR)
        gather(vector_copy, 0, SPECULAR, 1)
        gather(scalar_copy, 0, SPECULAR, 0)
        quantize(("dirs", 0, SPECULAR))
        quantize(("points", 0, SPECULAR))

        sort_words(scalar_copy, 1, 1)
        turn(1, 0)
        run_pass(0, 0, SPECULAR)
        gather(vector_copy, 1, 0, 0)
        gather(scalar_copy, 1, 0, 1)
        sort_words(vector_copy, 1, SPECULAR)
        turn(1, 1)
        for q in tiles_of(0):
            exponential(0, q)
        quantize(("points", 1, 0))
        run_pass(1, 0, 0)
        gather(vector_copy, 1, 1, 0)
        gather(scalar_copy, 1, 1, 1)
        turn(1, SPECULAR)
        times_cosine_gpsimd(0, 0)
        times_cosine_gpsimd(0, 1)
        times_cosine_vector(0, 2)
        times_cosine_gpsimd(0, 3)
        interleave_vector(1, 0)
        interleave_scalar(1, 0)
        quantize(("points", 1, 1))
        gather(vector_copy, 1, SPECULAR, 0)
        gather(scalar_copy, 1, SPECULAR, 1)
        zeros_bank = psum.tile([P, COLS], F32, name="turned")
        for i in range(2):
            nc.tensor.matmul_mx(
                out=zeros_bank[:],
                lhsT=codes[zeros][:, 0:P].bitcast(E4M3),
                lhsT_scale=scales[zeros][:, 0:P],
                rhs=codes[zeros][:].bitcast(E4M3),
                rhs_scale=scales[zeros][:],
                start=(i == 0),
                stop=(i == 1),
            )
        for q in tiles_of(0):
            turn_back(0, q)
        run_pass(1, 0, 1)
        interleave_vector(1, 1)
        interleave_scalar(1, 1)
        quantize(("points", 1, SPECULAR))
        interleave_vector(1, SPECULAR)
        interleave_scalar(1, SPECULAR)
        run_pass(1, 0, SPECULAR)
        for q in tiles_of(0):
            exponential(1, q)
        for g in range(PASSES):
            quantize(("dirs", 1, g))
        for q in (0, 1, 3):
            times_cosine_gpsimd(1, q)
        for q in tiles_of(0):
            times_light(0, q)
        store_rows(0, 0, 0, PACK)
        times_cosine_vector(1, 2)

        def prepare(i):
            for what, b, g in PREPARE.get(i, []):
                if what == "V":
                    interleave_vector(b, g)
                elif what == "S":
                    interleave_scalar(b, g)
                else:
                    quantize(("dirs", b, g))

        prepare(1)
        for i in range(2, len(RUNS) - 1):
            h, b = RUNS[i]
            for q in tiles_of(b):
                for g in range(PASSES):
                    unit_pass(h, q, g)
                exponential(h, q)
                times_cosine_gpsimd(h, q)
            h_before, b_before = RUNS[i - 1]
            for q in tiles_of(b_before):
                turn_back(h_before, q)
            if i == len(RUNS) - 2:
                for j in range(PACK):
                    make_light_cosine(nc.gpsimd if j == PACK - 1 else nc.vector, j)
            for q in tiles_of(b_before):
                times_light(h_before, q)
            store_rows(h_before, b_before, 0, PACK)
            prepare(i)

        h, b = RUNS[-2]
        last_unit(0)
        last_unit(1)
        for j in range(PACK):
            turn_back_row(h, b, j)
        last_unit(2)
        last_unit(3)
        last_exponential(0)
        last_exponential(1)
        times_light_row(h, b, 0)
        times_light_row(h, b, 1)
        store_rows(h, b, 0, 2)
        finish_last(nc.gpsimd, 0)
        finish_last(nc.gpsimd, 1)
        times_light_row(h, b, 2)
        last_exponential(2)
        times_light_row(h, b, 3)
        store_rows(h, b, 2, 4)
        last_exponential(3)
        finish_last(nc.vector, 2)
        finish_last(nc.vector, 3)
